import numpy as np
import ml_dtypes


def mxq(x, axis, fmt="e4m3"):
    dtype, down = {"e4m3": (ml_dtypes.float8_e4m3fn, 7), "e5m2": (ml_dtypes.float8_e5m2, 14)}[fmt]
    v = np.moveaxis(np.asarray(x, np.float32).astype(ml_dtypes.bfloat16).astype(np.float64), axis, -1)
    blocks = v.reshape(v.shape[:-1] + (-1, 32))
    amax = np.abs(blocks).max(-1, keepdims=True)
    byte = np.maximum(np.where(amax > 0, np.frexp(amax)[1] - 1 + 127, 0) - down, 1)
    scale = np.exp2(byte - 127.0)
    codes = (blocks / scale).astype(np.float32).astype(dtype).astype(np.float64)
    return np.moveaxis((codes * scale).reshape(v.shape), -1, axis)


WIDE = False


def mx_kscale(k):
    if not WIDE:
        return np.ones(k)
    levels = np.array([10, -10, 5, -5, 0])
    if k % 512:
        return np.exp2(np.random.permutation(np.resize(levels, k // 32))).repeat(32)
    a = np.empty((k // 512, 16))
    for p in range(k // 512):
        a[p, :8] = np.random.permutation(np.resize(levels, 8))
        for g in range(8):
            far = levels[np.abs(levels - a[p, g]) >= 10]
            a[p, g + 8] = far[np.random.randint(len(far))]
    return np.exp2(a.ravel()).repeat(32)


def f64(x):
    return np.asarray(x).astype(np.float64)


def striped8(idx):
    return np.asarray(idx).reshape(8, -1, 16).transpose(0, 2, 1).reshape(128, -1).astype(np.uint16)


def unstriped8(offs):
    return offs.reshape(8, 16, -1).transpose(0, 2, 1).reshape(8, -1).astype(np.int64)


def pick8(x, idx, run):
    r = np.arange(len(x))
    return x[r[:, None], idx[r % (8 * run) // run]]


E2M1 = np.array([0.0, 0.5, 1.0, 1.5, 2.0, 3.0, 4.0, 6.0, -0.0, -0.5, -1.0, -1.5, -2.0, -3.0, -4.0, -6.0])


def pack_weight(w, fmt):
    k, n = w.shape
    w = f64(np.asarray(w, np.float32).astype(ml_dtypes.bfloat16)).reshape(k // 32, 32, n)
    amax = np.abs(w).max(1)
    if fmt == "e4m3":
        byte = np.frexp(amax)[1] - 1 + 127 - 7
    else:
        mant, ex = np.frexp(amax / 6.0)
        byte = np.where(mant > 0.5, ex, ex - 1) + 127
    byte = np.clip(np.where(amax > 0, byte, 1), 1, 254)
    scaled = (w * np.exp2(127.0 - byte)[:, None, :]).reshape(k, n).astype(np.float32)
    by_word = np.ascontiguousarray(scaled.reshape(k // 512, 128, 4, n).transpose(0, 1, 3, 2))
    if fmt == "e4m3":
        words = by_word.astype(ml_dtypes.float8_e4m3fn).view(np.uint8)
    else:
        c = by_word.astype(ml_dtypes.float4_e2m1fn).view(np.uint8) & 0xF
        words = (c[..., 0::2] | (c[..., 1::2] << 4)).reshape(k // 512, 128, 2 * n)
    return np.ascontiguousarray(words), np.ascontiguousarray(byte.astype(np.uint8).reshape(k // 512, 16, n))


def unpack_weight(words, scales, fmt):
    g, _, n = scales.shape
    words = np.ascontiguousarray(words).reshape(g, 128, n, -1)
    if fmt == "e4m3":
        vals = words.view(ml_dtypes.float8_e4m3fn).astype(np.float64)
    else:
        nib = np.empty((g, 128, n, 4), np.uint8)
        nib[..., 0::2] = words & 0xF
        nib[..., 1::2] = words >> 4
        vals = E2M1[nib]
    vals = vals * np.repeat(np.exp2(scales.astype(np.float64) - 127.0), 8, axis=1)[..., None]
    return vals.transpose(0, 1, 3, 2).reshape(g * 512, n)


D, V, Q, I = 512, 2048, 128, 512


def setup_inputs():
    n = np.random.standard_normal
    idx = np.stack([np.random.permutation(V)[:I] for _ in range(8)])
    fd = mx_kscale(D)
    vocp = pack_weight(n((D, V)) / fd[:, None], "e2m1")
    return {
        "hid": (n((D, Q)) * 1.0 / np.sqrt(D) * fd[:, None]).astype(np.float32),
        "voc_words": vocp[0],
        "voc_scales": vocp[1],
        "mult": (np.random.uniform(100.0, 300.0, (Q, 1))).astype(np.float32),
        "sw": (np.random.uniform(0.005, 0.02, (1, I))).astype(np.float32),
        "old": (0.5 * n((Q, V))).astype(np.float32),
        "offs": striped8(idx),
    }


def reference(hid, voc_words, voc_scales, mult, sw, old, offs):
    idx = unstriped8(offs)
    vocu = unpack_weight(voc_words, voc_scales, "e2m1")
    hidq = mxq(f64(hid), 0, "e4m3")
    a = hidq.T @ vocu
    m1 = np.max(a, axis=1, keepdims=True)
    p = np.exp(a - m1)
    z = np.sum(p, axis=1, keepdims=True)
    px = np.exp(pick8(a, idx, 16) - m1)
    u1 = px / z
    du1 = f64(sw) * (1.0 - u1 * f64(mult)) / u1 + f64(sw) * np.log(u1) * (-1.0) * f64(mult)
    dpx = du1 / z
    dz = np.sum(du1 * px / np.square(z) * (-1.0), axis=1, keepdims=True)
    e1 = dpx * px
    s1 = np.zeros((Q, V))
    s1[np.arange(Q)[:, None], idx[np.arange(Q) % 128 // 16]] = e1
    da = dz * p + s1
    y = da * 64.0 + f64(old)
    return y

@@ -1,0 +1,258 @@
+import math
+from contextlib import ExitStack
+
+import concourse.mybir as mybir
+from concourse.masks import make_identity
+
+D, V, Q, I = 512, 2048, 128, 512
+FLOPS = 2 * D * V * Q
+
+F32 = mybir.dt.float32
+BF16 = mybir.dt.bfloat16
+I32 = mybir.dt.int32
+U32 = mybir.dt.uint32
+U16 = mybir.dt.uint16
+U8 = mybir.dt.uint8
+FP8X4 = mybir.dt.float8_e4m3fn_x4
+FP4X4 = mybir.dt.float4_e2m1fn_x4
+ALU = mybir.AluOpType
+ACT = mybir.ActivationFunctionType
+
+P = 128
+PACK = 4
+BANK = 512
+BANKS = V // BANK
+BLOCKS = BANK // P
+HALF = V // 2
+WIDTHS = [256, 256, 512, 512, 512]
+CHUNKS = len(WIDTHS)
+STARTS = [sum(WIDTHS[:c]) for c in range(CHUNKS)]
+NARROW = [0, 1]
+WIDE = [2, 3, 4]
+GRAD_SCALE = 64.0
+TERMS = 40
+EXPONENT_MASK = 0x7F800000
+LN2 = math.log(2.0)
+
+
+def tile_attend_bfocal_heads_kernel(tc, hid, voc_words, voc_scales, mult, sw, old, offs, out):
+    nc = tc.nc
+    with ExitStack() as ctx:
+        held = ctx.enter_context(tc.tile_pool(name="held", bufs=1))
+        psum = ctx.enter_context(tc.psum_pool(name="psum", bufs=1))
+
+        offsets = held.tile([P, I // 16], U16, name="offsets")
+        hid_raw = held.tile([P, PACK, Q], F32, name="hid_raw", tag="staging")
+        voc_plane = held.tile([P, V], U8, name="voc_plane", align_bytes=64)
+        words = held.tile([P, 2 * V], U8, name="words", align_bytes=64)
+        sw_quads = held.tile([P, PACK], F32, name="sw_quads", tag="codes", align_bytes=64)
+        scattered = held.tile([P, V], F32, name="scattered")
+
+        nc.vector.memset(voc_plane[:].bitcast(I32), 0)
+        nc.sync.dma_start(out=sw_quads[:], in_=sw.rearrange("o (p t) -> (o p) t", t=PACK))
+        nc.sync.dma_start(out=hid_raw[:], in_=hid.rearrange("(p t) q -> p t q", t=PACK))
+        for quad in range(4):
+            nc.scalar.dma_start(
+                out=voc_plane[32 * quad : 32 * quad + 4, :].bitcast(I32),
+                in_=voc_scales[0, 4 * quad : 4 * quad + 4, :].bitcast(I32),
+            )
+        nc.sync.dma_start(out=words[:].bitcast(I32), in_=voc_words[0].bitcast(I32))
+        nc.sync.dma_start(offsets[:], offs)
+
+        nc.vector.memset(scattered[:], 0.0)
+
+        identity = held.tile([P, P], F32, name="identity")
+        make_identity(nc, identity[:])
+
+        orders = held.tile([P, TERMS], F32, name="orders", tag="orders")
+        nc.gpsimd.iota(orders[:], [[-1, TERMS]], base=TERMS, channel_multiplier=0, allow_small_or_imprecise_dtypes=True)
+        series = held.tile([P, TERMS + 1], F32, name="series")
+        nc.vector.reciprocal(out=series[:, 0:TERMS], in_=orders[:])
+        mult_col = held.tile([P, 1], F32, name="mult_col", tag="orders")
+        nc.sync.dma_start(out=mult_col[:], in_=mult)
+
+        sw_bank = psum.tile([P, PACK, P], F32, name="sw_bank", tag="back0")
+        for t in range(PACK):
+            nc.tensor.transpose(sw_bank[:, t, :], sw_quads[:, t : t + 1].to_broadcast([P, P]), identity[:])
+        sw64 = held.tile([P, I], F32, name="sw64")
+        sw64_sum = held.tile([P, 1], F32, name="sw64_sum")
+        nc.scalar.activation(
+            out=sw64[:].rearrange("q (p t) -> q p t", t=PACK),
+            in_=sw_bank[:].rearrange("q t p -> q p t"),
+            func=ACT.Copy,
+            scale=GRAD_SCALE,
+            accum_out=sw64_sum[:],
+        )
+
+        hid_bf = held.tile([P, Q, PACK], BF16, name="hid_bf", align_bytes=64)
+        nc.vector.tensor_copy(
+            out=hid_bf[:].rearrange("p (c i) t -> p c t i", i=4),
+            in_=hid_raw[:].rearrange("p t (c i) -> p c t i", i=4),
+        )
+        old_sb = held.tile([P, V], F32, name="old_sb", tag="staging")
+        nc.sync.dma_start(out=old_sb[:], in_=old)
+        hid_codes = held.tile([P, Q], U32, name="hid_codes", tag="codes", align_bytes=64)
+        hid_plane = held.tile([P, Q], U8, name="hid_plane", align_bytes=64)
+        nc.vector.quantize_mx(
+            out=hid_codes[:].bitcast(FP8X4), scales=hid_plane[:], in_=hid_bf[:].rearrange("p q t -> p (q t)")
+        )
+
+        sw_mult = held.tile([P, I], F32, name="sw_mult")
+        nc.scalar.activation(out=sw_mult[:], in_=sw64[:], func=ACT.Copy, scale=mult_col[:])
+
+        scores = held.tile([P, V], F32, name="scores")
+        bank_max = held.tile([P, CHUNKS], F32, name="bank_max")
+        neg_max = held.tile([P, CHUNKS], F32, name="neg_max")
+        bank_sum = held.tile([P, CHUNKS], F32, name="bank_sum")
+        probs = [held.tile([P, WIDTHS[b]], F32, name=f"probs{b}") for b in range(CHUNKS)]
+        for b in range(CHUNKS):
+            cols = slice(STARTS[b], STARTS[b] + WIDTHS[b])
+            acc = psum.tile([P, WIDTHS[b]], F32, name=f"acc{b}", tag=f"acc{b}")
+            nc.tensor.matmul_mx(
+                out=acc[:],
+                lhsT=hid_codes[:].bitcast(FP8X4),
+                lhsT_scale=hid_plane[:],
+                rhs=words[:, 2 * STARTS[b] : 2 * (STARTS[b] + WIDTHS[b])].bitcast(FP4X4),
+                rhs_scale=voc_plane[:, cols],
+                start=True,
+                stop=True,
+            )
+            nc.vector.tensor_scalar(
+                out=scores[:, cols], in0=acc[:], scalar1=1.0, scalar2=None,
+                op0=ALU.mult, op1=ALU.max, accum_out=bank_max[:, b : b + 1],
+            )
+            if b == 0:
+                nc.gpsimd.tensor_scalar(
+                    out=neg_max[:, 0:1], in0=bank_max[:, 0:1], scalar1=-1.0, scalar2=0.0, op0=ALU.mult, op1=ALU.add
+                )
+            else:
+                nc.gpsimd.tensor_scalar(
+                    out=neg_max[:, b : b + 1], in0=bank_max[:, b : b + 1], scalar1=-1.0,
+                    scalar2=neg_max[:, b - 1 : b], op0=ALU.mult, op1=ALU.min,
+                )
+            nc.scalar.activation(
+                out=probs[b][:], in_=scores[:, cols], func=ACT.Exp, bias=neg_max[:, b : b + 1],
+                accum_out=bank_sum[:, b : b + 1],
+            )
+        neg_row_max = neg_max[:, CHUNKS - 1 : CHUNKS]
+
+        picked = held.tile([P, I], F32, name="picked")
+        nc.vector.tensor_copy(out=picked[:], in_=scores[:].indirect(offsets[:]))
+
+        rescale = held.tile([P, CHUNKS], F32, name="rescale")
+        nc.scalar.activation(out=rescale[:], in_=neg_max[:], func=ACT.Exp, scale=-1.0, bias=neg_row_max)
+        shift = held.tile([P, 1], F32, name="shift")
+        nc.gpsimd.tensor_scalar(
+            out=shift[:], in0=neg_row_max, scalar1=-1.0, scalar2=-1.0 - 127.0 * LN2,
+            op0=ALU.mult, op1=ALU.add,
+        )
+        picked_exp = held.tile([P, I], F32, name="picked_exp")
+        nc.scalar.activation(out=picked_exp[:], in_=picked[:], func=ACT.Exp, bias=neg_row_max)
+
+        neg_parts = held.tile([P, CHUNKS], F32, name="neg_parts")
+        neg_z = held.tile([P, 1], F32, name="neg_z")
+        nc.vector.scalar_tensor_tensor(
+            out=neg_parts[:], in0=bank_sum[:], scalar=-1.0, in1=rescale[:], op0=ALU.mult, op1=ALU.mult,
+            accum_out=neg_z[:],
+        )
+        neg_inv_z = held.tile([P, 1], F32, name="neg_inv_z")
+        nc.vector.reciprocal(out=neg_inv_z[:], in_=neg_z[:])
+        binade = held.tile([P, 1], I32, name="binade")
+        nc.vector.tensor_scalar(
+            out=binade[:], in0=neg_z[:].bitcast(I32), scalar1=EXPONENT_MASK, scalar2=None, op0=ALU.bitwise_and
+        )
+        gap = held.tile([P, TERMS + 1], F32, name="gap")
+        nc.vector.tensor_scalar(
+            out=gap[:], in0=neg_inv_z[:].to_broadcast([P, TERMS + 1]), scalar1=binade[:].bitcast(F32),
+            scalar2=1.0, op0=ALU.mult, op1=ALU.add,
+        )
+        nc.vector.tensor_scalar(
+            out=series[:, TERMS : TERMS + 1], in0=binade[:], scalar1=LN2 / 2.0**23, scalar2=shift[:],
+            op0=ALU.mult, op1=ALU.add,
+        )
+        horner = held.tile([P, TERMS + 1], F32, name="horner")
+        nc.vector.tensor_tensor_scan(
+            out=horner[:], data0=gap[:], data1=series[:], initial=0.0, op0=ALU.mult, op1=ALU.add
+        )
+        log_shift = horner[:, TERMS : TERMS + 1]
+
+        weighted = held.tile([P, I], F32, name="weighted")
+        nc.vector.scalar_tensor_tensor(
+            out=weighted[:], in0=picked_exp[:], scalar=neg_inv_z[:], in1=sw_mult[:], op0=ALU.mult, op1=ALU.mult
+        )
+        focal = held.tile([P, I], F32, name="focal")
+        focal_sum = held.tile([P, 1], F32, name="focal_sum")
+        nc.vector.scalar_tensor_tensor(
+            out=focal[:], in0=picked[:], scalar=log_shift, in1=weighted[:], op0=ALU.subtract, op1=ALU.mult,
+            accum_out=focal_sum[:],
+        )
+        nc.vector.tensor_tensor(out=scattered[:].indirect(offsets[:]), in0=focal[:], in1=sw64[:], op=ALU.add)
+
+        share = held.tile([P, CHUNKS], F32, name="share")
+        nc.scalar.activation(out=share[:], in_=rescale[:], func=ACT.Copy, scale=neg_inv_z[:])
+        share_sw = held.tile([P, CHUNKS], F32, name="share_sw")
+        nc.scalar.activation(out=share_sw[:], in_=share[:], func=ACT.Copy, scale=sw64_sum[:])
+        coef = held.tile([P, CHUNKS], F32, name="coef")
+        for b in WIDE + NARROW:
+            nc.scalar.activation(
+                out=coef[:, b : b + 1], in_=focal_sum[:], func=ACT.Identity,
+                scale=share[:, b : b + 1], bias=share_sw[:, b : b + 1],
+            )
+
+        def old_cols(start, width):
+            return old_sb[:, start : start + width]
+
+        turned = {b: psum.tile([P, BANK], F32, name=f"turned{b}", tag=f"acc{b}") for b in WIDE}
+        for b in WIDE:
+            for j in range(BLOCKS):
+                nc.tensor.matmul(
+                    turned[b][:, P * j : P * (j + 1)], lhsT=old_cols(STARTS[b] + P * j, P), rhs=identity[:],
+                    is_transpose=True, start=(j == 0), stop=False,
+                )
+
+        def scale_probs(b):
+            dense = held.tile([P, BANK], F32, name=f"dense{b}")
+            nc.scalar.activation(out=dense[:], in_=probs[b][:], func=ACT.Copy, scale=coef[:, b : b + 1])
+            for j in range(BLOCKS):
+                nc.tensor.matmul(
+                    turned[b][:, P * j : P * (j + 1)], lhsT=dense[:, P * j : P * (j + 1)], rhs=identity[:],
+                    is_transpose=True, start=False, stop=(j == BLOCKS - 1),
+                )
+
+        def turn_back(b):
+            turned_sb = held.tile([P, BANK], F32, name=f"turned_sb{b}")
+            nc.scalar.copy(out=turned_sb[:], in_=turned[b][:])
+            back = psum.tile([P, BANK], F32, name=f"back{b}", tag=f"back{b - WIDE[0]}")
+            for j in range(BLOCKS):
+                nc.tensor.transpose(back[:, P * j : P * (j + 1)], turned_sb[:, P * j : P * (j + 1)], identity[:])
+            return back
+
+        def finish_wide(b, back):
+            cols = slice(STARTS[b], STARTS[b] + BANK)
+            result = held.tile([P, BANK], F32, name=f"result{b}")
+            nc.vector.tensor_tensor(out=result[:], in0=back[:], in1=scattered[:, cols], op=ALU.add)
+            nc.sync.dma_start(out=out[:, cols], in_=result[:])
+
+        def add_old(b):
+            cols = slice(STARTS[b], STARTS[b] + WIDTHS[b])
+            partial = held.tile([P, WIDTHS[b]], F32, name=f"partial{b}")
+            nc.gpsimd.tensor_tensor(out=partial[:], in0=scattered[:, cols], in1=old_cols(STARTS[b], WIDTHS[b]), op=ALU.add)
+            return partial
+
+        def finish_narrow(b, partial):
+            cols = slice(STARTS[b], STARTS[b] + WIDTHS[b])
+            result = held.tile([P, WIDTHS[b]], F32, name=f"result{b}")
+            nc.vector.scalar_tensor_tensor(
+                out=result[:], in0=probs[b][:], scalar=coef[:, b : b + 1], in1=partial[:], op0=ALU.mult, op1=ALU.add
+            )
+            nc.sync.dma_start(out=out[:, cols], in_=result[:])
+
+        for b in WIDE:
+            scale_probs(b)
+        backs = {b: turn_back(b) for b in WIDE}
+        partials = {b: add_old(b) for b in NARROW}
+        finish_wide(WIDE[0], backs[WIDE[0]])
+        finish_narrow(NARROW[0], partials[NARROW[0]])
+        for b in WIDE[1:]:
+            finish_wide(b, backs[b])
+        finish_narrow(NARROW[1], partials[NARROW[1]])

@@ -27,8 +27,10 @@ HALF = V // 2
 WIDTHS = [256, 256, 512, 512, 512]
 CHUNKS = len(WIDTHS)
 STARTS = [sum(WIDTHS[:c]) for c in range(CHUNKS)]
-NARROW = [0, 1]
-WIDE = [2, 3, 4]
+POOLED = 2
+UNIT = 256
+UNITS = [(b, u) for b in range(CHUNKS) if b != POOLED for u in range(0, WIDTHS[b], UNIT)]
+LEAD = 3
 GRAD_SCALE = 64.0
 TERMS = 40
 EXPONENT_MASK = 0x7F800000
@@ -49,8 +51,8 @@ def tile_attend_bfocal_heads_kernel(tc, hid, voc_words, voc_scales, mult, sw, ol
         scattered = held.tile([P, V], F32, name="scattered")
 
         nc.vector.memset(voc_plane[:].bitcast(I32), 0)
-        nc.sync.dma_start(out=sw_quads[:], in_=sw.rearrange("o (p t) -> (o p) t", t=PACK))
         nc.sync.dma_start(out=hid_raw[:], in_=hid.rearrange("(p t) q -> p t q", t=PACK))
+        nc.sync.dma_start(out=sw_quads[:], in_=sw.rearrange("o (p t) -> (o p) t", t=PACK))
         for quad in range(4):
             nc.scalar.dma_start(
                 out=voc_plane[32 * quad : 32 * quad + 4, :].bitcast(I32),
@@ -59,19 +61,22 @@ def tile_attend_bfocal_heads_kernel(tc, hid, voc_words, voc_scales, mult, sw, ol
         nc.sync.dma_start(out=words[:].bitcast(I32), in_=voc_words[0].bitcast(I32))
         nc.sync.dma_start(offsets[:], offs)
 
+        ones = held.tile([P, TERMS], F32, name="ones", tag="ones")
+        nc.vector.memset(ones[:], 1.0)
         nc.vector.memset(scattered[:], 0.0)
+        orders = held.tile([P, TERMS], F32, name="orders")
+        nc.vector.tensor_tensor_scan(
+            out=orders[:], data0=ones[:], data1=ones[:], initial=TERMS + 1.0, op0=ALU.mult, op1=ALU.subtract
+        )
+        series = held.tile([P, TERMS + 1], F32, name="series")
+        nc.vector.reciprocal(out=series[:, 0:TERMS], in_=orders[:])
+        mult_col = held.tile([P, 1], F32, name="mult_col", tag="ones")
+        nc.sync.dma_start(out=mult_col[:], in_=mult)
 
         identity = held.tile([P, P], F32, name="identity")
         make_identity(nc, identity[:])
 
-        orders = held.tile([P, TERMS], F32, name="orders", tag="orders")
-        nc.gpsimd.iota(orders[:], [[-1, TERMS]], base=TERMS, channel_multiplier=0, allow_small_or_imprecise_dtypes=True)
-        series = held.tile([P, TERMS + 1], F32, name="series")
-        nc.vector.reciprocal(out=series[:, 0:TERMS], in_=orders[:])
-        mult_col = held.tile([P, 1], F32, name="mult_col", tag="orders")
-        nc.sync.dma_start(out=mult_col[:], in_=mult)
-
-        sw_bank = psum.tile([P, PACK, P], F32, name="sw_bank", tag="back0")
+        sw_bank = psum.tile([P, PACK, P], F32, name="sw_bank", tag="spare0")
         for t in range(PACK):
             nc.tensor.transpose(sw_bank[:, t, :], sw_quads[:, t : t + 1].to_broadcast([P, P]), identity[:])
         sw64 = held.tile([P, I], F32, name="sw64")
@@ -97,12 +102,11 @@ def tile_attend_bfocal_heads_kernel(tc, hid, voc_words, voc_scales, mult, sw, ol
             out=hid_codes[:].bitcast(FP8X4), scales=hid_plane[:], in_=hid_bf[:].rearrange("p q t -> p (q t)")
         )
 
-        sw_mult = held.tile([P, I], F32, name="sw_mult")
-        nc.scalar.activation(out=sw_mult[:], in_=sw64[:], func=ACT.Copy, scale=mult_col[:])
-
         scores = held.tile([P, V], F32, name="scores")
         bank_max = held.tile([P, CHUNKS], F32, name="bank_max")
         neg_max = held.tile([P, CHUNKS], F32, name="neg_max")
+        neg_row_max = neg_max[:, CHUNKS - 1 : CHUNKS]
+        rescale = held.tile([P, CHUNKS], F32, name="rescale")
         bank_sum = held.tile([P, CHUNKS], F32, name="bank_sum")
         probs = [held.tile([P, WIDTHS[b]], F32, name=f"probs{b}") for b in range(CHUNKS)]
         for b in range(CHUNKS):
@@ -130,17 +134,16 @@ def tile_attend_bfocal_heads_kernel(tc, hid, voc_words, voc_scales, mult, sw, ol
                     out=neg_max[:, b : b + 1], in0=bank_max[:, b : b + 1], scalar1=-1.0,
                     scalar2=neg_max[:, b - 1 : b], op0=ALU.mult, op1=ALU.min,
                 )
+            if b == CHUNKS - 1:
+                nc.scalar.activation(out=rescale[:], in_=neg_max[:], func=ACT.Exp, scale=-1.0, bias=neg_row_max)
             nc.scalar.activation(
                 out=probs[b][:], in_=scores[:, cols], func=ACT.Exp, bias=neg_max[:, b : b + 1],
                 accum_out=bank_sum[:, b : b + 1],
             )
-        neg_row_max = neg_max[:, CHUNKS - 1 : CHUNKS]
 
         picked = held.tile([P, I], F32, name="picked")
         nc.vector.tensor_copy(out=picked[:], in_=scores[:].indirect(offsets[:]))
 
-        rescale = held.tile([P, CHUNKS], F32, name="rescale")
-        nc.scalar.activation(out=rescale[:], in_=neg_max[:], func=ACT.Exp, scale=-1.0, bias=neg_row_max)
         shift = held.tile([P, 1], F32, name="shift")
         nc.gpsimd.tensor_scalar(
             out=shift[:], in0=neg_row_max, scalar1=-1.0, scalar2=-1.0 - 127.0 * LN2,
@@ -161,6 +164,8 @@ def tile_attend_bfocal_heads_kernel(tc, hid, voc_words, voc_scales, mult, sw, ol
         nc.vector.tensor_scalar(
             out=binade[:], in0=neg_z[:].bitcast(I32), scalar1=EXPONENT_MASK, scalar2=None, op0=ALU.bitwise_and
         )
+        slope = held.tile([P, 1], F32, name="slope")
+        nc.vector.tensor_tensor(out=slope[:], in0=neg_inv_z[:], in1=mult_col[:], op=ALU.mult)
         gap = held.tile([P, TERMS + 1], F32, name="gap")
         nc.vector.tensor_scalar(
             out=gap[:], in0=neg_inv_z[:].to_broadcast([P, TERMS + 1]), scalar1=binade[:].bitcast(F32),
@@ -170,16 +175,16 @@ def tile_attend_bfocal_heads_kernel(tc, hid, voc_words, voc_scales, mult, sw, ol
             out=series[:, TERMS : TERMS + 1], in0=binade[:], scalar1=LN2 / 2.0**23, scalar2=shift[:],
             op0=ALU.mult, op1=ALU.add,
         )
+        weighted = held.tile([P, I], F32, name="weighted")
+        nc.vector.scalar_tensor_tensor(
+            out=weighted[:], in0=picked_exp[:], scalar=slope[:], in1=sw64[:], op0=ALU.mult, op1=ALU.mult
+        )
         horner = held.tile([P, TERMS + 1], F32, name="horner")
         nc.vector.tensor_tensor_scan(
             out=horner[:], data0=gap[:], data1=series[:], initial=0.0, op0=ALU.mult, op1=ALU.add
         )
         log_shift = horner[:, TERMS : TERMS + 1]
 
-        weighted = held.tile([P, I], F32, name="weighted")
-        nc.vector.scalar_tensor_tensor(
-            out=weighted[:], in0=picked_exp[:], scalar=neg_inv_z[:], in1=sw_mult[:], op0=ALU.mult, op1=ALU.mult
-        )
         focal = held.tile([P, I], F32, name="focal")
         focal_sum = held.tile([P, 1], F32, name="focal_sum")
         nc.vector.scalar_tensor_tensor(
@@ -193,66 +198,66 @@ def tile_attend_bfocal_heads_kernel(tc, hid, voc_words, voc_scales, mult, sw, ol
         share_sw = held.tile([P, CHUNKS], F32, name="share_sw")
         nc.scalar.activation(out=share_sw[:], in_=share[:], func=ACT.Copy, scale=sw64_sum[:])
         coef = held.tile([P, CHUNKS], F32, name="coef")
-        for b in WIDE + NARROW:
+        for b in range(CHUNKS):
             nc.scalar.activation(
                 out=coef[:, b : b + 1], in_=focal_sum[:], func=ACT.Identity,
                 scale=share[:, b : b + 1], bias=share_sw[:, b : b + 1],
             )
 
-        def old_cols(start, width):
-            return old_sb[:, start : start + width]
+        blocks = [slice(P * j, P * (j + 1)) for j in range(UNIT // P)]
+        back_tags = ["spare1", "spare2", "spare0", "acc1", "acc2", "acc3"]
+        turned = {}
 
-        turned = {b: psum.tile([P, BANK], F32, name=f"turned{b}", tag=f"acc{b}") for b in WIDE}
-        for b in WIDE:
-            for j in range(BLOCKS):
+        def turn_old(k):
+            b, u = UNITS[k]
+            turned[k] = psum.tile([P, UNIT], F32, name=f"turned{k}", tag=f"acc{k % CHUNKS}")
+            old_unit = old_sb[:, STARTS[b] + u : STARTS[b] + u + UNIT]
+            for j, block in enumerate(blocks):
                 nc.tensor.matmul(
-                    turned[b][:, P * j : P * (j + 1)], lhsT=old_cols(STARTS[b] + P * j, P), rhs=identity[:],
+                    turned[k][:, block], lhsT=old_unit[:, block], rhs=identity[:],
                     is_transpose=True, start=(j == 0), stop=False,
                 )
 
-        def scale_probs(b):
-            dense = held.tile([P, BANK], F32, name=f"dense{b}")
-            nc.scalar.activation(out=dense[:], in_=probs[b][:], func=ACT.Copy, scale=coef[:, b : b + 1])
-            for j in range(BLOCKS):
+        for k in range(CHUNKS):
+            turn_old(k)
+
+        def scale_unit(k):
+            b, u = UNITS[k]
+            if k >= CHUNKS:
+                turn_old(k)
+            dense = held.tile([P, UNIT], F32, name=f"dense{k}")
+            nc.scalar.activation(out=dense[:], in_=probs[b][:, u : u + UNIT], func=ACT.Copy, scale=coef[:, b : b + 1])
+            for j, block in enumerate(blocks):
                 nc.tensor.matmul(
-                    turned[b][:, P * j : P * (j + 1)], lhsT=dense[:, P * j : P * (j + 1)], rhs=identity[:],
-                    is_transpose=True, start=False, stop=(j == BLOCKS - 1),
+                    turned[k][:, block], lhsT=dense[:, block], rhs=identity[:],
+                    is_transpose=True, start=False, stop=(j == len(blocks) - 1),
                 )
 
-        def turn_back(b):
-            turned_sb = held.tile([P, BANK], F32, name=f"turned_sb{b}")
-            nc.scalar.copy(out=turned_sb[:], in_=turned[b][:])
-            back = psum.tile([P, BANK], F32, name=f"back{b}", tag=f"back{b - WIDE[0]}")
-            for j in range(BLOCKS):
-                nc.tensor.transpose(back[:, P * j : P * (j + 1)], turned_sb[:, P * j : P * (j + 1)], identity[:])
-            return back
-
-        def finish_wide(b, back):
-            cols = slice(STARTS[b], STARTS[b] + BANK)
-            result = held.tile([P, BANK], F32, name=f"result{b}")
+        def finish_unit(k):
+            b, u = UNITS[k]
+            cols = slice(STARTS[b] + u, STARTS[b] + u + UNIT)
+            turned_sb = held.tile([P, UNIT], F32, name=f"turned_sb{k}", tag=f"turned_sb{k}")
+            nc.scalar.copy(out=turned_sb[:], in_=turned[k][:])
+            back = psum.tile([P, UNIT], F32, name=f"back{k}", tag=back_tags[k])
+            for block in blocks:
+                nc.tensor.transpose(back[:, block], turned_sb[:, block], identity[:])
+            result = held.tile([P, UNIT], F32, name=f"result{k}")
             nc.vector.tensor_tensor(out=result[:], in0=back[:], in1=scattered[:, cols], op=ALU.add)
             nc.sync.dma_start(out=out[:, cols], in_=result[:])
 
-        def add_old(b):
-            cols = slice(STARTS[b], STARTS[b] + WIDTHS[b])
-            partial = held.tile([P, WIDTHS[b]], F32, name=f"partial{b}")
-            nc.gpsimd.tensor_tensor(out=partial[:], in0=scattered[:, cols], in1=old_cols(STARTS[b], WIDTHS[b]), op=ALU.add)
-            return partial
+        for k in range(len(UNITS) + LEAD):
+            if k >= LEAD:
+                finish_unit(k - LEAD)
+            if k < len(UNITS):
+                scale_unit(k)
 
-        def finish_narrow(b, partial):
-            cols = slice(STARTS[b], STARTS[b] + WIDTHS[b])
-            result = held.tile([P, WIDTHS[b]], F32, name=f"result{b}")
+        pooled_cols = slice(STARTS[POOLED], STARTS[POOLED] + WIDTHS[POOLED])
+        partial = held.tile([P, WIDTHS[POOLED]], F32, name="partial")
+        nc.gpsimd.tensor_tensor(out=partial[:], in0=scattered[:, pooled_cols], in1=old_sb[:, pooled_cols], op=ALU.add)
+        for h, u in enumerate(range(0, WIDTHS[POOLED], UNIT)):
+            result = held.tile([P, UNIT], F32, name=f"pooled_result{h}", tag=f"turned_sb{len(UNITS) - 1 - h}")
             nc.vector.scalar_tensor_tensor(
-                out=result[:], in0=probs[b][:], scalar=coef[:, b : b + 1], in1=partial[:], op0=ALU.mult, op1=ALU.add
+                out=result[:], in0=probs[POOLED][:, u : u + UNIT], scalar=coef[:, POOLED : POOLED + 1],
+                in1=partial[:, u : u + UNIT], op0=ALU.mult, op1=ALU.add,
             )
-            nc.sync.dma_start(out=out[:, cols], in_=result[:])
-
-        for b in WIDE:
-            scale_probs(b)
-        backs = {b: turn_back(b) for b in WIDE}
-        partials = {b: add_old(b) for b in NARROW}
-        finish_wide(WIDE[0], backs[WIDE[0]])
-        finish_narrow(NARROW[0], partials[NARROW[0]])
-        for b in WIDE[1:]:
-            finish_wide(b, backs[b])
-        finish_narrow(NARROW[1], partials[NARROW[1]])
+            nc.sync.dma_start(out=out[:, STARTS[POOLED] + u : STARTS[POOLED] + u + UNIT], in_=result[:])

@@ -30,7 +30,7 @@ STARTS = [sum(WIDTHS[:c]) for c in range(CHUNKS)]
 POOLED = 2
 UNIT = 256
 UNITS = [(b, u) for b in range(CHUNKS) if b != POOLED for u in range(0, WIDTHS[b], UNIT)]
-LEAD = 3
+LEAD = 4
 GRAD_SCALE = 64.0
 TERMS = 40
 EXPONENT_MASK = 0x7F800000
@@ -104,9 +104,10 @@ def tile_attend_bfocal_heads_kernel(tc, hid, voc_words, voc_scales, mult, sw, ol
 
         scores = held.tile([P, V], F32, name="scores")
         bank_max = held.tile([P, CHUNKS], F32, name="bank_max")
-        neg_max = held.tile([P, CHUNKS], F32, name="neg_max")
-        neg_row_max = neg_max[:, CHUNKS - 1 : CHUNKS]
+        neg_max = held.tile([P, CHUNKS - 1], F32, name="neg_max")
+        neg_row_max = held.tile([P, 1], F32, name="neg_row_max")[:]
         rescale = held.tile([P, CHUNKS], F32, name="rescale")
+        nc.vector.memset(rescale[:], 1.0)
         bank_sum = held.tile([P, CHUNKS], F32, name="bank_sum")
         probs = [held.tile([P, WIDTHS[b]], F32, name=f"probs{b}") for b in range(CHUNKS)]
         for b in range(CHUNKS):
@@ -122,22 +123,22 @@ def tile_attend_bfocal_heads_kernel(tc, hid, voc_words, voc_scales, mult, sw, ol
                 stop=True,
             )
             nc.vector.tensor_scalar(
-                out=scores[:, cols], in0=acc[:], scalar1=1.0, scalar2=None,
+                out=scores[:, cols], in0=acc[:], scalar1=1.0, scalar2=bank_max[:, b - 2 : b - 1] if b >= 2 else None,
                 op0=ALU.mult, op1=ALU.max, accum_out=bank_max[:, b : b + 1],
             )
-            if b == 0:
+            if b < CHUNKS - 1:
                 nc.gpsimd.tensor_scalar(
-                    out=neg_max[:, 0:1], in0=bank_max[:, 0:1], scalar1=-1.0, scalar2=0.0, op0=ALU.mult, op1=ALU.add
+                    out=neg_max[:, b : b + 1], in0=bank_max[:, b : b + 1], scalar1=-1.0, scalar2=0.0,
+                    op0=ALU.mult, op1=ALU.add,
                 )
             else:
-                nc.gpsimd.tensor_scalar(
-                    out=neg_max[:, b : b + 1], in0=bank_max[:, b : b + 1], scalar1=-1.0,
-                    scalar2=neg_max[:, b - 1 : b], op0=ALU.mult, op1=ALU.min,
+                nc.vector.tensor_scalar(
+                    out=neg_row_max, in0=bank_max[:, b : b + 1], scalar1=bank_max[:, b - 1 : b], scalar2=-1.0,
+                    op0=ALU.max, op1=ALU.mult,
                 )
-            if b == CHUNKS - 1:
-                nc.scalar.activation(out=rescale[:], in_=neg_max[:], func=ACT.Exp, scale=-1.0, bias=neg_row_max)
+                nc.scalar.activation(out=rescale[:, 0:b], in_=neg_max[:], func=ACT.Exp, scale=-1.0, bias=neg_row_max)
             nc.scalar.activation(
-                out=probs[b][:], in_=scores[:, cols], func=ACT.Exp, bias=neg_max[:, b : b + 1],
+                out=probs[b][:], in_=scores[:, cols], func=ACT.Exp, bias=neg_max[:, b : b + 1] if b < CHUNKS - 1 else neg_row_max,
                 accum_out=bank_sum[:, b : b + 1],
             )
 
@@ -145,7 +146,7 @@ def tile_attend_bfocal_heads_kernel(tc, hid, voc_words, voc_scales, mult, sw, ol
         nc.vector.tensor_copy(out=picked[:], in_=scores[:].indirect(offsets[:]))
 
         shift = held.tile([P, 1], F32, name="shift")
-        nc.gpsimd.tensor_scalar(
+        nc.vector.tensor_scalar(
             out=shift[:], in0=neg_row_max, scalar1=-1.0, scalar2=-1.0 - 127.0 * LN2,
             op0=ALU.mult, op1=ALU.add,
         )
@@ -233,6 +234,8 @@ def tile_attend_bfocal_heads_kernel(tc, hid, voc_words, voc_scales, mult, sw, ol
                     is_transpose=True, start=False, stop=(j == len(blocks) - 1),
                 )
 
+        result = held.tile([P, V], F32, name="result")
+
         def finish_unit(k):
             b, u = UNITS[k]
             cols = slice(STARTS[b] + u, STARTS[b] + u + UNIT)
@@ -241,9 +244,10 @@ def tile_attend_bfocal_heads_kernel(tc, hid, voc_words, voc_scales, mult, sw, ol
             back = psum.tile([P, UNIT], F32, name=f"back{k}", tag=back_tags[k])
             for block in blocks:
                 nc.tensor.transpose(back[:, block], turned_sb[:, block], identity[:])
-            result = held.tile([P, UNIT], F32, name=f"result{k}")
-            nc.vector.tensor_tensor(out=result[:], in0=back[:], in1=scattered[:, cols], op=ALU.add)
-            nc.sync.dma_start(out=out[:, cols], in_=result[:])
+            nc.vector.tensor_tensor(out=result[:, cols], in0=back[:], in1=scattered[:, cols], op=ALU.add)
+            if k % 2 == 1:
+                pair = slice(cols.stop - 2 * UNIT, cols.stop)
+                nc.sync.dma_start(out=out[:, pair], in_=result[:, pair])
 
         for k in range(len(UNITS) + LEAD):
             if k >= LEAD:
@@ -255,9 +259,9 @@ def tile_attend_bfocal_heads_kernel(tc, hid, voc_words, voc_scales, mult, sw, ol
         partial = held.tile([P, WIDTHS[POOLED]], F32, name="partial")
         nc.gpsimd.tensor_tensor(out=partial[:], in0=scattered[:, pooled_cols], in1=old_sb[:, pooled_cols], op=ALU.add)
         for h, u in enumerate(range(0, WIDTHS[POOLED], UNIT)):
-            result = held.tile([P, UNIT], F32, name=f"pooled_result{h}", tag=f"turned_sb{len(UNITS) - 1 - h}")
+            pooled_result = held.tile([P, UNIT], F32, name=f"pooled_result{h}", tag=f"turned_sb{len(UNITS) - 1 - h}")
             nc.vector.scalar_tensor_tensor(
-                out=result[:], in0=probs[POOLED][:, u : u + UNIT], scalar=coef[:, POOLED : POOLED + 1],
+                out=pooled_result[:], in0=probs[POOLED][:, u : u + UNIT], scalar=coef[:, POOLED : POOLED + 1],
                 in1=partial[:, u : u + UNIT], op0=ALU.mult, op1=ALU.add,
             )
-            nc.sync.dma_start(out=out[:, STARTS[POOLED] + u : STARTS[POOLED] + u + UNIT], in_=result[:])
+            nc.sync.dma_start(out=out[:, STARTS[POOLED] + u : STARTS[POOLED] + u + UNIT], in_=pooled_result[:])

@@ -46,7 +46,7 @@ def tile_attend_bfocal_heads_kernel(tc, hid, voc_words, voc_scales, mult, sw, ol
         offsets = held.tile([P, I // 16], U16, name="offsets")
         hid_raw = held.tile([P, PACK, Q], F32, name="hid_raw", tag="staging")
         voc_plane = held.tile([P, V], U8, name="voc_plane", align_bytes=64)
-        words = held.tile([P, 2 * V], U8, name="words", align_bytes=64)
+        words_a = held.tile([P, V], U8, name="words_a", tag="words_a", align_bytes=64)
         sw_quads = held.tile([P, PACK], F32, name="sw_quads", tag="codes", align_bytes=64)
         scattered = held.tile([P, V], F32, name="scattered")
 
@@ -58,10 +58,10 @@ def tile_attend_bfocal_heads_kernel(tc, hid, voc_words, voc_scales, mult, sw, ol
                 out=voc_plane[32 * quad : 32 * quad + 4, :].bitcast(I32),
                 in_=voc_scales[0, 4 * quad : 4 * quad + 4, :].bitcast(I32),
             )
-        nc.sync.dma_start(out=words[:].bitcast(I32), in_=voc_words[0].bitcast(I32))
+        nc.sync.dma_start(out=words_a[:].bitcast(I32), in_=voc_words[0, :, 0:V].bitcast(I32))
         nc.sync.dma_start(offsets[:], offs)
 
-        ones = held.tile([P, TERMS], F32, name="ones", tag="ones")
+        ones = held.tile([P, TERMS], F32, name="ones", tag="words_b", align_bytes=64)
         nc.vector.memset(ones[:], 1.0)
         nc.vector.memset(scattered[:], 0.0)
         orders = held.tile([P, TERMS], F32, name="orders")
@@ -70,8 +70,9 @@ def tile_attend_bfocal_heads_kernel(tc, hid, voc_words, voc_scales, mult, sw, ol
         )
         series = held.tile([P, TERMS + 1], F32, name="series")
         nc.vector.reciprocal(out=series[:, 0:TERMS], in_=orders[:])
-        mult_col = held.tile([P, 1], F32, name="mult_col", tag="ones")
-        nc.sync.dma_start(out=mult_col[:], in_=mult)
+        words_b = held.tile([P, V], U8, name="words_b", tag="words_b", align_bytes=64)
+        nc.sync.dma_start(out=words_b[:].bitcast(I32), in_=voc_words[0, :, V : 2 * V].bitcast(I32))
+        words = [words_a, words_b]
 
         identity = held.tile([P, P], F32, name="identity")
         make_identity(nc, identity[:])
@@ -113,11 +114,12 @@ def tile_attend_bfocal_heads_kernel(tc, hid, voc_words, voc_scales, mult, sw, ol
         for b in range(CHUNKS):
             cols = slice(STARTS[b], STARTS[b] + WIDTHS[b])
             acc = psum.tile([P, WIDTHS[b]], F32, name=f"acc{b}", tag=f"acc{b}")
+            byte0 = 2 * (STARTS[b] % HALF)
             nc.tensor.matmul_mx(
                 out=acc[:],
                 lhsT=hid_codes[:].bitcast(FP8X4),
                 lhsT_scale=hid_plane[:],
-                rhs=words[:, 2 * STARTS[b] : 2 * (STARTS[b] + WIDTHS[b])].bitcast(FP4X4),
+                rhs=words[STARTS[b] // HALF][:, byte0 : byte0 + 2 * WIDTHS[b]].bitcast(FP4X4),
                 rhs_scale=voc_plane[:, cols],
                 start=True,
                 stop=True,
@@ -141,6 +143,9 @@ def tile_attend_bfocal_heads_kernel(tc, hid, voc_words, voc_scales, mult, sw, ol
                 out=probs[b][:], in_=scores[:, cols], func=ACT.Exp, bias=neg_max[:, b : b + 1] if b < CHUNKS - 1 else neg_row_max,
                 accum_out=bank_sum[:, b : b + 1],
             )
+
+        mult_col = held.tile([P, 1], F32, name="mult_col", tag="words_a", align_bytes=64)
+        nc.sync.dma_start(out=mult_col[:], in_=mult)
 
         picked = held.tile([P, I], F32, name="picked")
         nc.vector.tensor_copy(out=picked[:], in_=scores[:].indirect(offsets[:]))

import math
from contextlib import ExitStack

import concourse.mybir as mybir
from concourse.masks import make_identity

D, V, Q, I = 512, 2048, 128, 512
FLOPS = 2 * D * V * Q

F32 = mybir.dt.float32
BF16 = mybir.dt.bfloat16
I32 = mybir.dt.int32
U32 = mybir.dt.uint32
U16 = mybir.dt.uint16
U8 = mybir.dt.uint8
FP8X4 = mybir.dt.float8_e4m3fn_x4
FP4X4 = mybir.dt.float4_e2m1fn_x4
ALU = mybir.AluOpType
ACT = mybir.ActivationFunctionType

P = 128
PACK = 4
BANK = 512
BANKS = V // BANK
BLOCKS = BANK // P
HALF = V // 2
WIDTHS = [256, 256, 512, 512, 512]
CHUNKS = len(WIDTHS)
STARTS = [sum(WIDTHS[:c]) for c in range(CHUNKS)]
POOLED = 2
UNIT = 256
UNITS = [(b, u) for b in range(CHUNKS) if b != POOLED for u in range(0, WIDTHS[b], UNIT)]
LEAD = 4
GRAD_SCALE = 64.0
TERMS = 40
EXPONENT_MASK = 0x7F800000
LN2 = math.log(2.0)


def tile_attend_bfocal_heads_kernel(tc, hid, voc_words, voc_scales, mult, sw, old, offs, out):
    nc = tc.nc
    with ExitStack() as ctx:
        held = ctx.enter_context(tc.tile_pool(name="held", bufs=1))
        psum = ctx.enter_context(tc.psum_pool(name="psum", bufs=1))

        offsets = held.tile([P, I // 16], U16, name="offsets")
        hid_raw = held.tile([P, PACK, Q], F32, name="hid_raw", tag="staging")
        voc_plane = held.tile([P, V], U8, name="voc_plane", align_bytes=64)
        words_a = held.tile([P, V], U8, name="words_a", tag="words_a", align_bytes=64)
        sw_quads = held.tile([P, PACK], F32, name="sw_quads", tag="codes", align_bytes=64)
        scattered = held.tile([P, V], F32, name="scattered")

        nc.vector.memset(voc_plane[:].bitcast(I32), 0)
        nc.sync.dma_start(out=hid_raw[:], in_=hid.rearrange("(p t) q -> p t q", t=PACK))
        nc.sync.dma_start(out=sw_quads[:], in_=sw.rearrange("o (p t) -> (o p) t", t=PACK))
        for quad in range(4):
            nc.scalar.dma_start(
                out=voc_plane[32 * quad : 32 * quad + 4, :].bitcast(I32),
                in_=voc_scales[0, 4 * quad : 4 * quad + 4, :].bitcast(I32),
            )
        nc.sync.dma_start(out=words_a[:].bitcast(I32), in_=voc_words[0, :, 0:V].bitcast(I32))
        nc.sync.dma_start(offsets[:], offs)

        ones = held.tile([P, TERMS], F32, name="ones", tag="words_b", align_bytes=64)
        nc.vector.memset(ones[:], 1.0)
        nc.vector.memset(scattered[:], 0.0)
        orders = held.tile([P, TERMS], F32, name="orders")
        nc.vector.tensor_tensor_scan(
            out=orders[:], data0=ones[:], data1=ones[:], initial=TERMS + 1.0, op0=ALU.mult, op1=ALU.subtract
        )
        series = held.tile([P, TERMS + 1], F32, name="series")
        nc.vector.reciprocal(out=series[:, 0:TERMS], in_=orders[:])
        words_b = held.tile([P, V], U8, name="words_b", tag="words_b", align_bytes=64)
        nc.sync.dma_start(out=words_b[:].bitcast(I32), in_=voc_words[0, :, V : 2 * V].bitcast(I32))
        words = [words_a, words_b]

        identity = held.tile([P, P], F32, name="identity")
        make_identity(nc, identity[:])

        sw_bank = psum.tile([P, PACK, P], F32, name="sw_bank", tag="spare0")
        for t in range(PACK):
            nc.tensor.transpose(sw_bank[:, t, :], sw_quads[:, t : t + 1].to_broadcast([P, P]), identity[:])
        sw64 = held.tile([P, I], F32, name="sw64")
        sw64_sum = held.tile([P, 1], F32, name="sw64_sum")
        nc.scalar.activation(
            out=sw64[:].rearrange("q (p t) -> q p t", t=PACK),
            in_=sw_bank[:].rearrange("q t p -> q p t"),
            func=ACT.Copy,
            scale=GRAD_SCALE,
            accum_out=sw64_sum[:],
        )

        hid_bf = held.tile([P, Q, PACK], BF16, name="hid_bf", align_bytes=64)
        nc.vector.tensor_copy(
            out=hid_bf[:].rearrange("p (c i) t -> p c t i", i=4),
            in_=hid_raw[:].rearrange("p t (c i) -> p c t i", i=4),
        )
        old_sb = held.tile([P, V], F32, name="old_sb", tag="staging")
        nc.sync.dma_start(out=old_sb[:], in_=old)
        hid_codes = held.tile([P, Q], U32, name="hid_codes", tag="codes", align_bytes=64)
        hid_plane = held.tile([P, Q], U8, name="hid_plane", align_bytes=64)
        nc.vector.quantize_mx(
            out=hid_codes[:].bitcast(FP8X4), scales=hid_plane[:], in_=hid_bf[:].rearrange("p q t -> p (q t)")
        )

        scores = held.tile([P, V], F32, name="scores")
        bank_max = held.tile([P, CHUNKS], F32, name="bank_max")
        neg_max = held.tile([P, CHUNKS - 1], F32, name="neg_max")
        neg_row_max = held.tile([P, 1], F32, name="neg_row_max")[:]
        rescale = held.tile([P, CHUNKS], F32, name="rescale")
        nc.vector.memset(rescale[:], 1.0)
        bank_sum = held.tile([P, CHUNKS], F32, name="bank_sum")
        probs = [held.tile([P, WIDTHS[b]], F32, name=f"probs{b}") for b in range(CHUNKS)]
        for b in range(CHUNKS):
            cols = slice(STARTS[b], STARTS[b] + WIDTHS[b])
            acc = psum.tile([P, WIDTHS[b]], F32, name=f"acc{b}", tag=f"acc{b}")
            byte0 = 2 * (STARTS[b] % HALF)
            nc.tensor.matmul_mx(
                out=acc[:],
                lhsT=hid_codes[:].bitcast(FP8X4),
                lhsT_scale=hid_plane[:],
                rhs=words[STARTS[b] // HALF][:, byte0 : byte0 + 2 * WIDTHS[b]].bitcast(FP4X4),
                rhs_scale=voc_plane[:, cols],
                start=True,
                stop=True,
            )
            nc.vector.tensor_scalar(
                out=scores[:, cols], in0=acc[:], scalar1=1.0, scalar2=bank_max[:, b - 2 : b - 1] if b >= 2 else None,
                op0=ALU.mult, op1=ALU.max, accum_out=bank_max[:, b : b + 1],
            )
            if b < CHUNKS - 1:
                nc.gpsimd.tensor_scalar(
                    out=neg_max[:, b : b + 1], in0=bank_max[:, b : b + 1], scalar1=-1.0, scalar2=0.0,
                    op0=ALU.mult, op1=ALU.add,
                )
            else:
                nc.vector.tensor_scalar(
                    out=neg_row_max, in0=bank_max[:, b : b + 1], scalar1=bank_max[:, b - 1 : b], scalar2=-1.0,
                    op0=ALU.max, op1=ALU.mult,
                )
                nc.scalar.activation(out=rescale[:, 0:b], in_=neg_max[:], func=ACT.Exp, scale=-1.0, bias=neg_row_max)
            nc.scalar.activation(
                out=probs[b][:], in_=scores[:, cols], func=ACT.Exp, bias=neg_max[:, b : b + 1] if b < CHUNKS - 1 else neg_row_max,
                accum_out=bank_sum[:, b : b + 1],
            )

        mult_col = held.tile([P, 1], F32, name="mult_col", tag="words_a", align_bytes=64)
        nc.sync.dma_start(out=mult_col[:], in_=mult)

        picked = held.tile([P, I], F32, name="picked")
        nc.vector.tensor_copy(out=picked[:], in_=scores[:].indirect(offsets[:]))

        shift = held.tile([P, 1], F32, name="shift")
        nc.vector.tensor_scalar(
            out=shift[:], in0=neg_row_max, scalar1=-1.0, scalar2=-1.0 - 127.0 * LN2,
            op0=ALU.mult, op1=ALU.add,
        )
        picked_exp = held.tile([P, I], F32, name="picked_exp")
        nc.scalar.activation(out=picked_exp[:], in_=picked[:], func=ACT.Exp, bias=neg_row_max)

        neg_parts = held.tile([P, CHUNKS], F32, name="neg_parts")
        neg_z = held.tile([P, 1], F32, name="neg_z")
        nc.vector.scalar_tensor_tensor(
            out=neg_parts[:], in0=bank_sum[:], scalar=-1.0, in1=rescale[:], op0=ALU.mult, op1=ALU.mult,
            accum_out=neg_z[:],
        )
        neg_inv_z = held.tile([P, 1], F32, name="neg_inv_z")
        nc.vector.reciprocal(out=neg_inv_z[:], in_=neg_z[:])
        binade = held.tile([P, 1], I32, name="binade")
        nc.vector.tensor_scalar(
            out=binade[:], in0=neg_z[:].bitcast(I32), scalar1=EXPONENT_MASK, scalar2=None, op0=ALU.bitwise_and
        )
        slope = held.tile([P, 1], F32, name="slope")
        nc.vector.tensor_tensor(out=slope[:], in0=neg_inv_z[:], in1=mult_col[:], op=ALU.mult)
        gap = held.tile([P, TERMS + 1], F32, name="gap")
        nc.vector.tensor_scalar(
            out=gap[:], in0=neg_inv_z[:].to_broadcast([P, TERMS + 1]), scalar1=binade[:].bitcast(F32),
            scalar2=1.0, op0=ALU.mult, op1=ALU.add,
        )
        nc.vector.tensor_scalar(
            out=series[:, TERMS : TERMS + 1], in0=binade[:], scalar1=LN2 / 2.0**23, scalar2=shift[:],
            op0=ALU.mult, op1=ALU.add,
        )
        weighted = held.tile([P, I], F32, name="weighted")
        nc.vector.scalar_tensor_tensor(
            out=weighted[:], in0=picked_exp[:], scalar=slope[:], in1=sw64[:], op0=ALU.mult, op1=ALU.mult
        )
        horner = held.tile([P, TERMS + 1], F32, name="horner")
        nc.vector.tensor_tensor_scan(
            out=horner[:], data0=gap[:], data1=series[:], initial=0.0, op0=ALU.mult, op1=ALU.add
        )
        log_shift = horner[:, TERMS : TERMS + 1]

        focal = held.tile([P, I], F32, name="focal")
        focal_sum = held.tile([P, 1], F32, name="focal_sum")
        nc.vector.scalar_tensor_tensor(
            out=focal[:], in0=picked[:], scalar=log_shift, in1=weighted[:], op0=ALU.subtract, op1=ALU.mult,
            accum_out=focal_sum[:],
        )
        nc.vector.tensor_tensor(out=scattered[:].indirect(offsets[:]), in0=focal[:], in1=sw64[:], op=ALU.add)

        share = held.tile([P, CHUNKS], F32, name="share")
        nc.scalar.activation(out=share[:], in_=rescale[:], func=ACT.Copy, scale=neg_inv_z[:])
        share_sw = held.tile([P, CHUNKS], F32, name="share_sw")
        nc.scalar.activation(out=share_sw[:], in_=share[:], func=ACT.Copy, scale=sw64_sum[:])
        coef = held.tile([P, CHUNKS], F32, name="coef")
        for b in range(CHUNKS):
            nc.scalar.activation(
                out=coef[:, b : b + 1], in_=focal_sum[:], func=ACT.Identity,
                scale=share[:, b : b + 1], bias=share_sw[:, b : b + 1],
            )

        blocks = [slice(P * j, P * (j + 1)) for j in range(UNIT // P)]
        back_tags = ["spare1", "spare2", "spare0", "acc1", "acc2", "acc3"]
        turned = {}

        def turn_old(k):
            b, u = UNITS[k]
            turned[k] = psum.tile([P, UNIT], F32, name=f"turned{k}", tag=f"acc{k % CHUNKS}")
            old_unit = old_sb[:, STARTS[b] + u : STARTS[b] + u + UNIT]
            for j, block in enumerate(blocks):
                nc.tensor.matmul(
                    turned[k][:, block], lhsT=old_unit[:, block], rhs=identity[:],
                    is_transpose=True, start=(j == 0), stop=False,
                )

        for k in range(CHUNKS):
            turn_old(k)

        def scale_unit(k):
            b, u = UNITS[k]
            if k >= CHUNKS:
                turn_old(k)
            dense = held.tile([P, UNIT], F32, name=f"dense{k}")
            nc.scalar.activation(out=dense[:], in_=probs[b][:, u : u + UNIT], func=ACT.Copy, scale=coef[:, b : b + 1])
            for j, block in enumerate(blocks):
                nc.tensor.matmul(
                    turned[k][:, block], lhsT=dense[:, block], rhs=identity[:],
                    is_transpose=True, start=False, stop=(j == len(blocks) - 1),
                )

        result = held.tile([P, V], F32, name="result")

        def finish_unit(k):
            b, u = UNITS[k]
            cols = slice(STARTS[b] + u, STARTS[b] + u + UNIT)
            turned_sb = held.tile([P, UNIT], F32, name=f"turned_sb{k}", tag=f"turned_sb{k}")
            nc.scalar.copy(out=turned_sb[:], in_=turned[k][:])
            back = psum.tile([P, UNIT], F32, name=f"back{k}", tag=back_tags[k])
            for block in blocks:
                nc.tensor.transpose(back[:, block], turned_sb[:, block], identity[:])
            nc.vector.tensor_tensor(out=result[:, cols], in0=back[:], in1=scattered[:, cols], op=ALU.add)
            if k % 2 == 1:
                pair = slice(cols.stop - 2 * UNIT, cols.stop)
                nc.sync.dma_start(out=out[:, pair], in_=result[:, pair])

        for k in range(len(UNITS) + LEAD):
            if k >= LEAD:
                finish_unit(k - LEAD)
            if k < len(UNITS):
                scale_unit(k)

        pooled_cols = slice(STARTS[POOLED], STARTS[POOLED] + WIDTHS[POOLED])
        partial = held.tile([P, WIDTHS[POOLED]], F32, name="partial")
        nc.gpsimd.tensor_tensor(out=partial[:], in0=scattered[:, pooled_cols], in1=old_sb[:, pooled_cols], op=ALU.add)
        for h, u in enumerate(range(0, WIDTHS[POOLED], UNIT)):
            pooled_result = held.tile([P, UNIT], F32, name=f"pooled_result{h}", tag=f"turned_sb{len(UNITS) - 1 - h}")
            nc.vector.scalar_tensor_tensor(
                out=pooled_result[:], in0=probs[POOLED][:, u : u + UNIT], scalar=coef[:, POOLED : POOLED + 1],
                in1=partial[:, u : u + UNIT], op0=ALU.mult, op1=ALU.add,
            )
            nc.sync.dma_start(out=out[:, STARTS[POOLED] + u : STARTS[POOLED] + u + UNIT], in_=pooled_result[:])
